import numpy as np
import ml_dtypes


def mxq(x, axis, fmt="e4m3"):
    dtype, down = {"e4m3": (ml_dtypes.float8_e4m3fn, 7), "e5m2": (ml_dtypes.float8_e5m2, 14)}[fmt]
    v = np.moveaxis(np.asarray(x, np.float32).astype(ml_dtypes.bfloat16).astype(np.float64), axis, -1)
    blocks = v.reshape(v.shape[:-1] + (-1, 32))
    amax = np.abs(blocks).max(-1, keepdims=True)
    byte = np.maximum(np.where(amax > 0, np.frexp(amax)[1] - 1 + 127, 0) - down, 1)
    scale = np.exp2(byte - 127.0)
    codes = (blocks / scale).astype(np.float32).astype(dtype).astype(np.float64)
    return np.moveaxis((codes * scale).reshape(v.shape), -1, axis)


WIDE = False


def mx_kscale(k):
    if not WIDE:
        return np.ones(k)
    levels = np.array([10, -10, 5, -5, 0])
    if k % 512:
        return np.exp2(np.random.permutation(np.resize(levels, k // 32))).repeat(32)
    a = np.empty((k // 512, 16))
    for p in range(k // 512):
        a[p, :8] = np.random.permutation(np.resize(levels, 8))
        for g in range(8):
            far = levels[np.abs(levels - a[p, g]) >= 10]
            a[p, g + 8] = far[np.random.randint(len(far))]
    return np.exp2(a.ravel()).repeat(32)


def f64(x):
    return np.asarray(x).astype(np.float64)


def striped8(idx):
    return np.asarray(idx).reshape(8, -1, 16).transpose(0, 2, 1).reshape(128, -1).astype(np.uint16)


def unstriped8(offs):
    return offs.reshape(8, 16, -1).transpose(0, 2, 1).reshape(8, -1).astype(np.int64)


def pick8(x, idx, run):
    r = np.arange(len(x))
    return x[r[:, None], idx[r % (8 * run) // run]]


E2M1 = np.array([0.0, 0.5, 1.0, 1.5, 2.0, 3.0, 4.0, 6.0, -0.0, -0.5, -1.0, -1.5, -2.0, -3.0, -4.0, -6.0])


def pack_weight(w, fmt):
    k, n = w.shape
    w = f64(np.asarray(w, np.float32).astype(ml_dtypes.bfloat16)).reshape(k // 32, 32, n)
    amax = np.abs(w).max(1)
    if fmt == "e4m3":
        byte = np.frexp(amax)[1] - 1 + 127 - 7
    else:
        mant, ex = np.frexp(amax / 6.0)
        byte = np.where(mant > 0.5, ex, ex - 1) + 127
    byte = np.clip(np.where(amax > 0, byte, 1), 1, 254)
    scaled = (w * np.exp2(127.0 - byte)[:, None, :]).reshape(k, n).astype(np.float32)
    by_word = np.ascontiguousarray(scaled.reshape(k // 512, 128, 4, n).transpose(0, 1, 3, 2))
    if fmt == "e4m3":
        words = by_word.astype(ml_dtypes.float8_e4m3fn).view(np.uint8)
    else:
        c = by_word.astype(ml_dtypes.float4_e2m1fn).view(np.uint8) & 0xF
        words = (c[..., 0::2] | (c[..., 1::2] << 4)).reshape(k // 512, 128, 2 * n)
    return np.ascontiguousarray(words), np.ascontiguousarray(byte.astype(np.uint8).reshape(k // 512, 16, n))


def unpack_weight(words, scales, fmt):
    g, _, n = scales.shape
    words = np.ascontiguousarray(words).reshape(g, 128, n, -1)
    if fmt == "e4m3":
        vals = words.view(ml_dtypes.float8_e4m3fn).astype(np.float64)
    else:
        nib = np.empty((g, 128, n, 4), np.uint8)
        nib[..., 0::2] = words & 0xF
        nib[..., 1::2] = words >> 4
        vals = E2M1[nib]
    vals = vals * np.repeat(np.exp2(scales.astype(np.float64) - 127.0), 8, axis=1)[..., None]
    return vals.transpose(0, 1, 3, 2).reshape(g * 512, n)


D, T, I, Q = 512, 1024, 512, 128


def setup_inputs():
    n = np.random.standard_normal
    idx = np.stack([np.random.permutation(T)[:I] for _ in range(8)])
    idx2 = np.stack([np.random.permutation(T)[:I] for _ in range(8)])
    idx3 = np.stack([np.random.permutation(T)[:I] for _ in range(8)])
    idx4 = np.stack([np.random.permutation(T)[:I] for _ in range(8)])
    fd = mx_kscale(D)
    keysp = pack_weight(n((D, T)) / fd[:, None], "e2m1")
    return {
        "query": (n((D, Q)) * 0.9 / np.sqrt(D) * fd[:, None]).astype(np.float32),
        "query2": (n((D, Q)) * 0.9 / np.sqrt(D) * fd[:, None]).astype(np.float32),
        "keys_words": keysp[0],
        "keys_scales": keysp[1],
        "lam": (np.random.uniform(0.5, 1.3, (Q, 1))).astype(np.float32),
        "old": (1.0 * n((Q, T))).astype(np.float32),
        "offs": striped8(idx),
        "offs2": striped8(idx2),
        "offs3": striped8(idx3),
        "offs4": striped8(idx4),
    }


def reference(query, query2, keys_words, keys_scales, lam, old, offs, offs2, offs3, offs4):
    idx = unstriped8(offs)
    idx2 = unstriped8(offs2)
    idx3 = unstriped8(offs3)
    idx4 = unstriped8(offs4)
    keysu = unpack_weight(keys_words, keys_scales, "e2m1")
    queryq = mxq(f64(query), 0, "e4m3")
    a = queryq.T @ keysu
    query2q = mxq(f64(query2), 0, "e4m3")
    b = query2q.T @ keysu
    w = (np.maximum(pick8(a, idx, 16), pick8(b, idx2, 16)) - np.maximum(pick8(a, idx2, 16), pick8(b, idx, 16))) * f64(lam)
    f1 = np.zeros((Q, T))
    f1[np.arange(Q)[:, None], idx[np.arange(Q) % 128 // 16]] = w
    f2 = f1 + f64(old)
    y = np.maximum(pick8(f2, idx3, 16), pick8(f2, idx4, 16))
    return y

@@ -1,0 +1,133 @@
+from contextlib import ExitStack
+
+import concourse.mybir as mybir
+
+D, T, I, Q = 512, 1024, 512, 128
+FLOPS = 2 * 2 * D * T * Q
+
+F32 = mybir.dt.float32
+BF16 = mybir.dt.bfloat16
+I32 = mybir.dt.int32
+U32 = mybir.dt.uint32
+U16 = mybir.dt.uint16
+U8 = mybir.dt.uint8
+FP8X4 = mybir.dt.float8_e4m3fn_x4
+FP4X4 = mybir.dt.float4_e2m1fn_x4
+ALU = mybir.AluOpType
+COPY = mybir.ActivationFunctionType.Copy
+
+P = 128
+PACK = 4
+N_PASS = 256
+HALF = I // 2
+LIST_COLS = HALF // 16
+
+
+def tile_attend_exchanged_lean_throughtwo_heads_kernel(
+    tc, query, query2, keys_words, keys_scales, lam, old, offs, offs2, offs3, offs4, out
+):
+    nc = tc.nc
+    with ExitStack() as ctx:
+        keep = ctx.enter_context(tc.tile_pool(name="keep", bufs=1))
+        psum = ctx.enter_context(tc.psum_pool(name="psum", bufs=1))
+
+        lists = [keep.tile([P, I // 16], U16, name=f"list{n}") for n in range(4)]
+        raw = [keep.tile([P, PACK, Q], F32, name=f"raw{n}") for n in range(2)]
+        words = keep.tile([P, 2 * T], U8, align_bytes=64)
+        kscales = keep.tile([P, T], U8, align_bytes=64)
+        lam_col = keep.tile([P, 1], F32)
+        old_sb = keep.tile([P, T], F32)
+        f1 = keep.tile([P, T], F32)
+
+        nc.vector.memset(kscales[:].bitcast(I32), 0)
+        nc.gpsimd.memset(f1[:], 0.0)
+
+        nc.sync.dma_start(out=raw[0][:], in_=query.rearrange("(p j) q -> p j q", j=PACK))
+        nc.sync.dma_start(out=words[:].bitcast(I32), in_=keys_words[0].bitcast(I32))
+        for quad in range(4):
+            nc.sync.dma_start(
+                out=kscales[32 * quad : 32 * quad + 4, :].bitcast(I32),
+                in_=keys_scales[0, 4 * quad : 4 * quad + 4, :].bitcast(I32),
+            )
+        nc.sync.dma_start(out=raw[1][:], in_=query2.rearrange("(p j) q -> p j q", j=PACK))
+        nc.sync.dma_start(lists[0][:], offs)
+        nc.sync.dma_start(lists[1][:], offs2)
+        nc.sync.dma_start(out=lam_col[:], in_=lam)
+        nc.sync.dma_start(out=old_sb[:], in_=old)
+        nc.sync.dma_start(lists[2][:], offs3)
+        nc.sync.dma_start(lists[3][:], offs4)
+
+        operands = []
+        for n in range(2):
+            grouped = keep.tile([P, Q, PACK], BF16, name=f"grouped{n}", align_bytes=64)
+            codes = keep.tile([P, Q], U32, name=f"codes{n}", align_bytes=64)
+            qscales = keep.tile([P, Q], U8, name=f"qscales{n}", align_bytes=64)
+            src = raw[n][:].rearrange("p j q -> p q j")
+            nc.vector.tensor_copy(out=grouped[:], in_=src)
+            nc.vector.quantize_mx(
+                out=codes[:].bitcast(FP8X4),
+                scales=qscales[:],
+                in_=grouped[:].rearrange("p q j -> p (q j)"),
+            )
+            operands.append((codes, qscales))
+        scores = []
+        for n, (codes, qscales) in enumerate(operands):
+            score = keep.tile([P, T], F32, name=f"score{n}")
+            for c0 in range(0, T, N_PASS):
+                acc = psum.tile([P, N_PASS], F32, name=f"acc{n}_{c0}")
+                nc.tensor.matmul_mx(
+                    out=acc[:],
+                    lhsT=codes[:].bitcast(FP8X4),
+                    lhsT_scale=qscales[:],
+                    rhs=words[:, 2 * c0 : 2 * (c0 + N_PASS)].bitcast(FP4X4),
+                    rhs_scale=kscales[:, c0 : c0 + N_PASS],
+                    start=True,
+                    stop=True,
+                )
+                if n == 0 and c0 == N_PASS:
+                    nc.vector.tensor_copy(score[:, c0 : c0 + N_PASS], acc[:])
+                else:
+                    nc.scalar.copy(score[:, c0 : c0 + N_PASS], acc[:])
+            scores.append(score)
+        a, b = scores
+
+        lam_wide = keep.tile([P, HALF], F32)
+        nc.vector.tensor_copy(out=lam_wide[:], in_=lam_col[:].to_broadcast([P, HALF]))
+
+
+        def half_of(lst, h):
+            return lst[:, h * LIST_COLS : (h + 1) * LIST_COLS]
+
+        def look_up(on_vector, name, table, offsets, tag=""):
+            got = keep.tile([P, HALF], F32, name=name, tag=tag or name)
+            if on_vector:
+                nc.vector.tensor_copy(got[:], table[:].indirect(offsets))
+            else:
+                nc.scalar.activation(got[:], table[:].indirect(offsets), COPY)
+            return got
+
+        for h in range(2):
+            first, second = half_of(lists[0], h), half_of(lists[1], h)
+            a1 = look_up(h == 0, f"a1_{h}", a, first)
+            a2 = look_up(h == 0, f"a2_{h}", a, second) if h == 0 else None
+            b2 = look_up(False, f"b2_{h}", b, second, "a2_0" if h == 1 else "")
+            if h == 1:
+                a2 = look_up(False, f"a2_{h}", a, second)
+            b1 = look_up(h == 0, f"b1_{h}", b, first, "m1_0" if h == 1 else "")
+            m1 = keep.tile([P, HALF], F32, name=f"m1_{h}", tag=f"m1_{h}")
+            m2 = keep.tile([P, HALF], F32, name=f"m2_{h}")
+            diff = keep.tile([P, HALF], F32, name=f"diff{h}")
+            nc.vector.tensor_tensor(m1[:], a1[:], b2[:], ALU.max)
+            nc.vector.tensor_tensor(m2[:], a2[:], b1[:], ALU.max)
+            nc.vector.tensor_tensor(diff[:], m1[:], m2[:], ALU.subtract)
+            nc.vector.tensor_tensor(f1[:].indirect(first), diff[:], lam_wide[:], ALU.mult)
+
+        f2 = keep.tile([P, T], F32)
+        nc.vector.tensor_tensor(f2[:], f1[:], old_sb[:], ALU.add)
+
+        third = [look_up(True, f"third{h}", f2, half_of(lists[2], h)) for h in range(2)]
+        fourth = [look_up(False, f"fourth{h}", f2, half_of(lists[3], h)) for h in range(2)]
+        for h in range(2):
+            res = keep.tile([P, HALF], F32, name=f"res{h}")
+            nc.vector.tensor_tensor(res[:], third[h][:], fourth[h][:], ALU.max)
+            nc.sync.dma_start(out=out[:, h * HALF : (h + 1) * HALF], in_=res[:])

@@ -20,7 +20,8 @@ P = 128
 PACK = 4
 N_PASS = 256
 HALF = I // 2
-LIST_COLS = HALF // 16
+QUARTER = I // 4
+Q_SCALAR = 80
 
 
 def tile_attend_exchanged_lean_throughtwo_heads_kernel(
@@ -63,7 +64,11 @@ def tile_attend_exchanged_lean_throughtwo_heads_kernel(
             codes = keep.tile([P, Q], U32, name=f"codes{n}", align_bytes=64)
             qscales = keep.tile([P, Q], U8, name=f"qscales{n}", align_bytes=64)
             src = raw[n][:].rearrange("p j q -> p q j")
-            nc.vector.tensor_copy(out=grouped[:], in_=src)
+            if n == 0:
+                nc.scalar.activation(grouped[:, :Q_SCALAR, :], src[:, :Q_SCALAR, :], COPY)
+                nc.vector.tensor_copy(out=grouped[:, Q_SCALAR:, :], in_=src[:, Q_SCALAR:, :])
+            else:
+                nc.vector.tensor_copy(out=grouped[:], in_=src)
             nc.vector.quantize_mx(
                 out=codes[:].bitcast(FP8X4),
                 scales=qscales[:],
@@ -84,43 +89,62 @@ def tile_attend_exchanged_lean_throughtwo_heads_kernel(
                     start=True,
                     stop=True,
                 )
-                if n == 0 and c0 == N_PASS:
-                    nc.vector.tensor_copy(score[:, c0 : c0 + N_PASS], acc[:])
-                else:
-                    nc.scalar.copy(score[:, c0 : c0 + N_PASS], acc[:])
+                nc.scalar.copy(score[:, c0 : c0 + N_PASS], acc[:])
             scores.append(score)
         a, b = scores
 
-        lam_wide = keep.tile([P, HALF], F32)
-        nc.vector.tensor_copy(out=lam_wide[:], in_=lam_col[:].to_broadcast([P, HALF]))
+        lam_wide = keep.tile([P, QUARTER], F32)
+        nc.vector.tensor_copy(out=lam_wide[:], in_=lam_col[:].to_broadcast([P, QUARTER]))
+        lam_neg = keep.tile([P, 1], F32)
+        nc.gpsimd.tensor_scalar(lam_neg[:], lam_col[:], -1.0, 0.0, ALU.mult, ALU.add)
 
+        def slots(lst, start, count):
+            return lst[:, start // 16 : (start + count) // 16]
 
         def half_of(lst, h):
-            return lst[:, h * LIST_COLS : (h + 1) * LIST_COLS]
+            return slots(lst, h * HALF, HALF)
 
-        def look_up(on_vector, name, table, offsets, tag=""):
-            got = keep.tile([P, HALF], F32, name=name, tag=tag or name)
+        def look_up(on_vector, name, table, offsets):
+            got = keep.tile([P, HALF], F32, name=name)
             if on_vector:
                 nc.vector.tensor_copy(got[:], table[:].indirect(offsets))
             else:
                 nc.scalar.activation(got[:], table[:].indirect(offsets), COPY)
             return got
 
-        for h in range(2):
-            first, second = half_of(lists[0], h), half_of(lists[1], h)
-            a1 = look_up(h == 0, f"a1_{h}", a, first)
-            a2 = look_up(h == 0, f"a2_{h}", a, second) if h == 0 else None
-            b2 = look_up(False, f"b2_{h}", b, second, "a2_0" if h == 1 else "")
-            if h == 1:
-                a2 = look_up(False, f"a2_{h}", a, second)
-            b1 = look_up(h == 0, f"b1_{h}", b, first, "m1_0" if h == 1 else "")
-            m1 = keep.tile([P, HALF], F32, name=f"m1_{h}", tag=f"m1_{h}")
-            m2 = keep.tile([P, HALF], F32, name=f"m2_{h}")
-            diff = keep.tile([P, HALF], F32, name=f"diff{h}")
-            nc.vector.tensor_tensor(m1[:], a1[:], b2[:], ALU.max)
-            nc.vector.tensor_tensor(m2[:], a2[:], b1[:], ALU.max)
-            nc.vector.tensor_tensor(diff[:], m1[:], m2[:], ALU.subtract)
-            nc.vector.tensor_tensor(f1[:].indirect(first), diff[:], lam_wide[:], ALU.mult)
+        def larger(name, x, y):
+            got = keep.tile([P, HALF], F32, name=name)
+            nc.vector.tensor_tensor(got[:], x[:], y[:], ALU.max)
+            return got
+
+        first, second = half_of(lists[0], 0), half_of(lists[1], 0)
+        a1 = look_up(True, "a1", a, first)
+        a2 = look_up(True, "a2", a, second)
+        b2 = look_up(False, "b2_lo", b, second)
+        b1 = look_up(True, "b1", b, first)
+        m1 = larger("m1_lo", a1, b2)
+        m2 = larger("m2_lo", a2, b1)
+        diff = keep.tile([P, HALF], F32)
+        nc.vector.tensor_tensor(diff[:], m1[:], m2[:], ALU.subtract)
+
+        first, second = half_of(lists[0], 1), half_of(lists[1], 1)
+        b2 = look_up(False, "b2_hi", b, second)
+        a1 = look_up(False, "a1", a, first)
+        a2 = look_up(False, "a2", a, second)
+        b1 = look_up(False, "b1", b, first)
+        m1 = larger("m1_hi", a1, b2)
+        nc.vector.tensor_tensor(
+            f1[:].indirect(slots(lists[0], 0, QUARTER)), diff[:, :QUARTER], lam_wide[:], ALU.mult
+        )
+        m2 = larger("m2_hi", a2, b1)
+        nc.vector.tensor_tensor(
+            f1[:].indirect(slots(lists[0], QUARTER, QUARTER)), diff[:, QUARTER:], lam_wide[:], ALU.mult
+        )
+        plus = keep.tile([P, HALF], F32)
+        minus = keep.tile([P, HALF], F32)
+        nc.scalar.activation(plus[:], m1[:], COPY, scale=lam_col[:])
+        nc.scalar.activation(minus[:], m2[:], COPY, scale=lam_neg[:])
+        nc.vector.tensor_tensor(f1[:].indirect(first), plus[:], minus[:], ALU.add)
 
         f2 = keep.tile([P, T], F32)
         nc.vector.tensor_tensor(f2[:], f1[:], old_sb[:], ALU.add)

@@ -41,7 +41,7 @@ def tile_attend_exchanged_lean_throughtwo_heads_kernel(
         f1 = keep.tile([P, T], F32)
 
         nc.vector.memset(kscales[:].bitcast(I32), 0)
-        nc.gpsimd.memset(f1[:], 0.0)
+        nc.vector.memset(f1[:], 0.0)
 
         nc.sync.dma_start(out=raw[0][:], in_=query.rearrange("(p j) q -> p j q", j=PACK))
         nc.sync.dma_start(out=words[:].bitcast(I32), in_=keys_words[0].bitcast(I32))
@@ -96,7 +96,7 @@ def tile_attend_exchanged_lean_throughtwo_heads_kernel(
         lam_wide = keep.tile([P, QUARTER], F32)
         nc.vector.tensor_copy(out=lam_wide[:], in_=lam_col[:].to_broadcast([P, QUARTER]))
         lam_neg = keep.tile([P, 1], F32)
-        nc.gpsimd.tensor_scalar(lam_neg[:], lam_col[:], -1.0, 0.0, ALU.mult, ALU.add)
+        nc.vector.tensor_scalar(lam_neg[:], lam_col[:], -1.0, 0.0, ALU.mult, ALU.add)
 
         def slots(lst, start, count):
             return lst[:, start // 16 : (start + count) // 16]
@@ -119,31 +119,31 @@ def tile_attend_exchanged_lean_throughtwo_heads_kernel(
 
         first, second = half_of(lists[0], 0), half_of(lists[1], 0)
         a1 = look_up(True, "a1", a, first)
-        a2 = look_up(True, "a2", a, second)
-        b2 = look_up(False, "b2_lo", b, second)
-        b1 = look_up(True, "b1", b, first)
-        m1 = larger("m1_lo", a1, b2)
-        m2 = larger("m2_lo", a2, b1)
+        a2 = look_up(True, "a2_lo", a, second)
+        b2 = look_up(False, "b2", b, second)
+        b1 = look_up(True, "b1_lo", b, first)
+        m2 = larger("m2", a2, b1)
+        m1 = larger("m1", a1, b2)
         diff = keep.tile([P, HALF], F32)
         nc.vector.tensor_tensor(diff[:], m1[:], m2[:], ALU.subtract)
 
         first, second = half_of(lists[0], 1), half_of(lists[1], 1)
-        b2 = look_up(False, "b2_hi", b, second)
+        a2 = look_up(False, "a2_hi", a, second)
+        b1 = look_up(False, "b1_hi", b, first)
         a1 = look_up(False, "a1", a, first)
-        a2 = look_up(False, "a2", a, second)
-        b1 = look_up(False, "b1", b, first)
-        m1 = larger("m1_hi", a1, b2)
+        b2 = look_up(False, "b2", b, second)
         nc.vector.tensor_tensor(
             f1[:].indirect(slots(lists[0], 0, QUARTER)), diff[:, :QUARTER], lam_wide[:], ALU.mult
         )
-        m2 = larger("m2_hi", a2, b1)
+        m2 = larger("m2", a2, b1)
+        m1 = larger("m1", a1, b2)
         nc.vector.tensor_tensor(
             f1[:].indirect(slots(lists[0], QUARTER, QUARTER)), diff[:, QUARTER:], lam_wide[:], ALU.mult
         )
         plus = keep.tile([P, HALF], F32)
         minus = keep.tile([P, HALF], F32)
-        nc.scalar.activation(plus[:], m1[:], COPY, scale=lam_col[:])
         nc.scalar.activation(minus[:], m2[:], COPY, scale=lam_neg[:])
+        nc.scalar.activation(plus[:], m1[:], COPY, scale=lam_col[:])
         nc.vector.tensor_tensor(f1[:].indirect(first), plus[:], minus[:], ALU.add)
 
         f2 = keep.tile([P, T], F32)

from contextlib import ExitStack

import concourse.mybir as mybir

D, T, I, Q = 512, 1024, 512, 128
FLOPS = 2 * 2 * D * T * Q

F32 = mybir.dt.float32
BF16 = mybir.dt.bfloat16
I32 = mybir.dt.int32
U32 = mybir.dt.uint32
U16 = mybir.dt.uint16
U8 = mybir.dt.uint8
FP8X4 = mybir.dt.float8_e4m3fn_x4
FP4X4 = mybir.dt.float4_e2m1fn_x4
ALU = mybir.AluOpType
COPY = mybir.ActivationFunctionType.Copy

P = 128
PACK = 4
N_PASS = 256
HALF = I // 2
QUARTER = I // 4
Q_SCALAR = 80


def tile_attend_exchanged_lean_throughtwo_heads_kernel(
    tc, query, query2, keys_words, keys_scales, lam, old, offs, offs2, offs3, offs4, out
):
    nc = tc.nc
    with ExitStack() as ctx:
        keep = ctx.enter_context(tc.tile_pool(name="keep", bufs=1))
        psum = ctx.enter_context(tc.psum_pool(name="psum", bufs=1))

        lists = [keep.tile([P, I // 16], U16, name=f"list{n}") for n in range(4)]
        raw = [keep.tile([P, PACK, Q], F32, name=f"raw{n}") for n in range(2)]
        words = keep.tile([P, 2 * T], U8, align_bytes=64)
        kscales = keep.tile([P, T], U8, align_bytes=64)
        lam_col = keep.tile([P, 1], F32)
        old_sb = keep.tile([P, T], F32)
        f1 = keep.tile([P, T], F32)

        nc.vector.memset(kscales[:].bitcast(I32), 0)
        nc.vector.memset(f1[:], 0.0)

        nc.sync.dma_start(out=raw[0][:], in_=query.rearrange("(p j) q -> p j q", j=PACK))
        nc.sync.dma_start(out=words[:].bitcast(I32), in_=keys_words[0].bitcast(I32))
        for quad in range(4):
            nc.sync.dma_start(
                out=kscales[32 * quad : 32 * quad + 4, :].bitcast(I32),
                in_=keys_scales[0, 4 * quad : 4 * quad + 4, :].bitcast(I32),
            )
        nc.sync.dma_start(out=raw[1][:], in_=query2.rearrange("(p j) q -> p j q", j=PACK))
        nc.sync.dma_start(lists[0][:], offs)
        nc.sync.dma_start(lists[1][:], offs2)
        nc.sync.dma_start(out=lam_col[:], in_=lam)
        nc.sync.dma_start(out=old_sb[:], in_=old)
        nc.sync.dma_start(lists[2][:], offs3)
        nc.sync.dma_start(lists[3][:], offs4)

        operands = []
        for n in range(2):
            grouped = keep.tile([P, Q, PACK], BF16, name=f"grouped{n}", align_bytes=64)
            codes = keep.tile([P, Q], U32, name=f"codes{n}", align_bytes=64)
            qscales = keep.tile([P, Q], U8, name=f"qscales{n}", align_bytes=64)
            src = raw[n][:].rearrange("p j q -> p q j")
            if n == 0:
                nc.scalar.activation(grouped[:, :Q_SCALAR, :], src[:, :Q_SCALAR, :], COPY)
                nc.vector.tensor_copy(out=grouped[:, Q_SCALAR:, :], in_=src[:, Q_SCALAR:, :])
            else:
                nc.vector.tensor_copy(out=grouped[:], in_=src)
            nc.vector.quantize_mx(
                out=codes[:].bitcast(FP8X4),
                scales=qscales[:],
                in_=grouped[:].rearrange("p q j -> p (q j)"),
            )
            operands.append((codes, qscales))
        scores = []
        for n, (codes, qscales) in enumerate(operands):
            score = keep.tile([P, T], F32, name=f"score{n}")
            for c0 in range(0, T, N_PASS):
                acc = psum.tile([P, N_PASS], F32, name=f"acc{n}_{c0}")
                nc.tensor.matmul_mx(
                    out=acc[:],
                    lhsT=codes[:].bitcast(FP8X4),
                    lhsT_scale=qscales[:],
                    rhs=words[:, 2 * c0 : 2 * (c0 + N_PASS)].bitcast(FP4X4),
                    rhs_scale=kscales[:, c0 : c0 + N_PASS],
                    start=True,
                    stop=True,
                )
                nc.scalar.copy(score[:, c0 : c0 + N_PASS], acc[:])
            scores.append(score)
        a, b = scores

        lam_wide = keep.tile([P, QUARTER], F32)
        nc.vector.tensor_copy(out=lam_wide[:], in_=lam_col[:].to_broadcast([P, QUARTER]))
        lam_neg = keep.tile([P, 1], F32)
        nc.vector.tensor_scalar(lam_neg[:], lam_col[:], -1.0, 0.0, ALU.mult, ALU.add)

        def slots(lst, start, count):
            return lst[:, start // 16 : (start + count) // 16]

        def half_of(lst, h):
            return slots(lst, h * HALF, HALF)

        def look_up(on_vector, name, table, offsets):
            got = keep.tile([P, HALF], F32, name=name)
            if on_vector:
                nc.vector.tensor_copy(got[:], table[:].indirect(offsets))
            else:
                nc.scalar.activation(got[:], table[:].indirect(offsets), COPY)
            return got

        def larger(name, x, y):
            got = keep.tile([P, HALF], F32, name=name)
            nc.vector.tensor_tensor(got[:], x[:], y[:], ALU.max)
            return got

        first, second = half_of(lists[0], 0), half_of(lists[1], 0)
        a1 = look_up(True, "a1", a, first)
        a2 = look_up(True, "a2_lo", a, second)
        b2 = look_up(False, "b2", b, second)
        b1 = look_up(True, "b1_lo", b, first)
        m2 = larger("m2", a2, b1)
        m1 = larger("m1", a1, b2)
        diff = keep.tile([P, HALF], F32)
        nc.vector.tensor_tensor(diff[:], m1[:], m2[:], ALU.subtract)

        first, second = half_of(lists[0], 1), half_of(lists[1], 1)
        a2 = look_up(False, "a2_hi", a, second)
        b1 = look_up(False, "b1_hi", b, first)
        a1 = look_up(False, "a1", a, first)
        b2 = look_up(False, "b2", b, second)
        nc.vector.tensor_tensor(
            f1[:].indirect(slots(lists[0], 0, QUARTER)), diff[:, :QUARTER], lam_wide[:], ALU.mult
        )
        m2 = larger("m2", a2, b1)
        m1 = larger("m1", a1, b2)
        nc.vector.tensor_tensor(
            f1[:].indirect(slots(lists[0], QUARTER, QUARTER)), diff[:, QUARTER:], lam_wide[:], ALU.mult
        )
        plus = keep.tile([P, HALF], F32)
        minus = keep.tile([P, HALF], F32)
        nc.scalar.activation(minus[:], m2[:], COPY, scale=lam_neg[:])
        nc.scalar.activation(plus[:], m1[:], COPY, scale=lam_col[:])
        nc.vector.tensor_tensor(f1[:].indirect(first), plus[:], minus[:], ALU.add)

        f2 = keep.tile([P, T], F32)
        nc.vector.tensor_tensor(f2[:], f1[:], old_sb[:], ALU.add)

        third = [look_up(True, f"third{h}", f2, half_of(lists[2], h)) for h in range(2)]
        fourth = [look_up(False, f"fourth{h}", f2, half_of(lists[3], h)) for h in range(2)]
        for h in range(2):
            res = keep.tile([P, HALF], F32, name=f"res{h}")
            nc.vector.tensor_tensor(res[:], third[h][:], fourth[h][:], ALU.max)
            nc.sync.dma_start(out=out[:, h * HALF : (h + 1) * HALF], in_=res[:])
